import numpy as np
import ml_dtypes


def mxq(x, axis, fmt="e4m3"):
    dtype, down = {"e4m3": (ml_dtypes.float8_e4m3fn, 7), "e5m2": (ml_dtypes.float8_e5m2, 14)}[fmt]
    v = np.moveaxis(np.asarray(x, np.float32).astype(ml_dtypes.bfloat16).astype(np.float64), axis, -1)
    blocks = v.reshape(v.shape[:-1] + (-1, 32))
    amax = np.abs(blocks).max(-1, keepdims=True)
    byte = np.maximum(np.where(amax > 0, np.frexp(amax)[1] - 1 + 127, 0) - down, 1)
    scale = np.exp2(byte - 127.0)
    codes = (blocks / scale).astype(np.float32).astype(dtype).astype(np.float64)
    return np.moveaxis((codes * scale).reshape(v.shape), -1, axis)


WIDE = False


def mx_kscale(k):
    if not WIDE:
        return np.ones(k)
    levels = np.array([10, -10, 5, -5, 0])
    if k % 512:
        return np.exp2(np.random.permutation(np.resize(levels, k // 32))).repeat(32)
    a = np.empty((k // 512, 16))
    for p in range(k // 512):
        a[p, :8] = np.random.permutation(np.resize(levels, 8))
        for g in range(8):
            far = levels[np.abs(levels - a[p, g]) >= 10]
            a[p, g + 8] = far[np.random.randint(len(far))]
    return np.exp2(a.ravel()).repeat(32)


def f64(x):
    return np.asarray(x).astype(np.float64)


def striped(idx):
    return np.tile(np.asarray(idx).reshape(-1, 16).T, (8, 1)).astype(np.uint16)


def unstriped(offs):
    return offs[:16].T.reshape(-1).astype(np.int64)


def striped8(idx):
    return np.asarray(idx).reshape(8, -1, 16).transpose(0, 2, 1).reshape(128, -1).astype(np.uint16)


def unstriped8(offs):
    return offs.reshape(8, 16, -1).transpose(0, 2, 1).reshape(8, -1).astype(np.int64)


def pick8(x, idx, run):
    r = np.arange(len(x))
    return x[r[:, None], idx[r % (8 * run) // run]]


E2M1 = np.array([0.0, 0.5, 1.0, 1.5, 2.0, 3.0, 4.0, 6.0, -0.0, -0.5, -1.0, -1.5, -2.0, -3.0, -4.0, -6.0])


def pack_weight(w, fmt):
    k, n = w.shape
    w = f64(np.asarray(w, np.float32).astype(ml_dtypes.bfloat16)).reshape(k // 32, 32, n)
    amax = np.abs(w).max(1)
    if fmt == "e4m3":
        byte = np.frexp(amax)[1] - 1 + 127 - 7
    else:
        mant, ex = np.frexp(amax / 6.0)
        byte = np.where(mant > 0.5, ex, ex - 1) + 127
    byte = np.clip(np.where(amax > 0, byte, 1), 1, 254)
    scaled = (w * np.exp2(127.0 - byte)[:, None, :]).reshape(k, n).astype(np.float32)
    by_word = np.ascontiguousarray(scaled.reshape(k // 512, 128, 4, n).transpose(0, 1, 3, 2))
    if fmt == "e4m3":
        words = by_word.astype(ml_dtypes.float8_e4m3fn).view(np.uint8)
    else:
        c = by_word.astype(ml_dtypes.float4_e2m1fn).view(np.uint8) & 0xF
        words = (c[..., 0::2] | (c[..., 1::2] << 4)).reshape(k // 512, 128, 2 * n)
    return np.ascontiguousarray(words), np.ascontiguousarray(byte.astype(np.uint8).reshape(k // 512, 16, n))


def unpack_weight(words, scales, fmt):
    g, _, n = scales.shape
    words = np.ascontiguousarray(words).reshape(g, 128, n, -1)
    if fmt == "e4m3":
        vals = words.view(ml_dtypes.float8_e4m3fn).astype(np.float64)
    else:
        nib = np.empty((g, 128, n, 4), np.uint8)
        nib[..., 0::2] = words & 0xF
        nib[..., 1::2] = words >> 4
        vals = E2M1[nib]
    vals = vals * np.repeat(np.exp2(scales.astype(np.float64) - 127.0), 8, axis=1)[..., None]
    return vals.transpose(0, 1, 3, 2).reshape(g * 512, n)


def sgn(shape):
    return np.random.uniform(0.5, 2.0, shape) * np.where(np.random.standard_normal(shape) < 0, -1.0, 1.0)


K, J, R, T, Z, M, O, N, U, E = 512, 512, 512, 2048, 512, 1024, 256, 256, 128, 512


def setup_inputs():
    n = np.random.standard_normal
    idx = np.stack([np.random.permutation(T)[:J] for _ in range(8)])
    idx2 = np.stack([np.random.permutation(T)[:J] for _ in range(8)])
    idx3 = np.random.permutation(M)[:J]
    idx4 = np.stack([np.random.permutation(J)[:O] for _ in range(8)])
    idx5 = np.stack([np.random.permutation(J)[:O] for _ in range(8)])
    idx6 = np.stack([np.random.permutation(O)[:U] for _ in range(8)])
    idx7 = np.stack([np.random.permutation(E)[:U] for _ in range(8)])
    fk = mx_kscale(K)
    fr = mx_kscale(R)
    fz = mx_kscale(Z)
    wp = pack_weight(n((K, R)) * 1 / np.sqrt(K) / fk[:, None] * fr, "e4m3")
    xop = pack_weight(n((Z, M)) / fz[:, None], "e4m3")
    w2p = pack_weight(n((Z, R)) * 1 / np.sqrt(Z) * fz[:, None] * fr, "e2m1")
    wbp = pack_weight(n((R, N)) * 1 / np.sqrt(R) / fr[:, None], "e2m1")
    return {
        "ta": (np.random.randint(-7, 8, (K, T)).astype(np.float64)).astype(np.float32),
        "ga": ((np.random.randint(10, 25, (K, 1)) / 64.0) * fk[:, None]).astype(np.float32),
        "gb": ((np.random.randint(4, 13, (K, 1)) / 64.0) * fk[:, None]).astype(np.float32),
        "w_words": wp[0],
        "w_scales": wp[1],
        "xo_words": xop[0],
        "xo_scales": xop[1],
        "w2_words": w2p[0],
        "w2_scales": w2p[1],
        "sa": (np.random.uniform(0.5, 1.6, (R, 1))).astype(np.float32),
        "sb": (np.random.uniform(0.5, 1.6, (R, 1))).astype(np.float32),
        "wb_words": wbp[0],
        "wb_scales": wbp[1],
        "so": (sgn((N, 1))).astype(np.float32),
        "offs": striped8(idx),
        "offs2": striped8(idx2),
        "offs3": striped(idx3),
        "offs4": striped8(idx4),
        "offs5": striped8(idx5),
        "offs6": striped8(idx6),
        "offs7": striped8(idx7),
    }


def reference(ta, ga, gb, w_words, w_scales, xo_words, xo_scales, w2_words, w2_scales, sa, sb, wb_words, wb_scales, so, offs, offs2, offs3, offs4, offs5, offs6, offs7):
    idx = unstriped8(offs)
    idx2 = unstriped8(offs2)
    idx3 = unstriped(offs3)
    idx4 = unstriped8(offs4)
    idx5 = unstriped8(offs5)
    idx6 = unstriped8(offs6)
    idx7 = unstriped8(offs7)
    wu = unpack_weight(w_words, w_scales, "e4m3")
    xou = unpack_weight(xo_words, xo_scales, "e4m3")
    w2u = unpack_weight(w2_words, w2_scales, "e2m1")
    wbu = unpack_weight(wb_words, wb_scales, "e2m1")
    xc = pick8(f64(ta), idx, 64) * f64(ga) + pick8(f64(ta), idx2, 64) * f64(gb)
    xcq = mxq(xc, 0, "e4m3")
    a = wu.T @ xcq
    xoidx3g = xou[:, idx3]
    b = w2u.T @ xoidx3g
    hid = np.maximum(pick8(a, idx4, 64) * f64(sa), pick8(b, idx5, 64) * f64(sb))
    hidq = mxq(hid, 0, "e4m3")
    p = wbu.T @ hidq
    m0 = pick8(p, idx6, 16) * f64(so)
    y = np.zeros((N, E))
    y[np.arange(N)[:, None], idx7[np.arange(N) % 128 // 16]] = m0
    return y

@@ -1,0 +1,294 @@
+from contextlib import ExitStack
+
+import concourse.mybir as mybir
+
+K, J, R, T, Z, M, O, N, U, E = 512, 512, 512, 2048, 512, 1024, 256, 256, 128, 512
+FLOPS = 2 * (K * R * J + Z * R * J + R * N * O)
+
+F32 = mybir.dt.float32
+BF16 = mybir.dt.bfloat16
+I32 = mybir.dt.int32
+U32 = mybir.dt.uint32
+U16 = mybir.dt.uint16
+U8 = mybir.dt.uint8
+FP8X4 = mybir.dt.float8_e4m3fn_x4
+FP4X4 = mybir.dt.float4_e2m1fn_x4
+COPY = mybir.ActivationFunctionType.Copy
+ADD = mybir.AluOpType.add
+MAX = mybir.AluOpType.max
+
+P = 128
+PACK = 4
+QUADS = 4
+BANK = 512
+
+
+def tile_picked_refined_plain_two_groupmeet_one_posted_kernel(
+    tc, ta, ga, gb, w_words, w_scales, xo_words, xo_scales, w2_words, w2_scales, sa, sb, wb_words, wb_scales, so,
+    offs, offs2, offs3, offs4, offs5, offs6, offs7, out,
+):
+    nc = tc.nc
+    with ExitStack() as ctx:
+        lists = ctx.enter_context(tc.tile_pool(name="lists", bufs=1))
+        keep = ctx.enter_context(tc.tile_pool(name="keep", bufs=1))
+        psum = ctx.enter_context(tc.psum_pool(name="psum", bufs=8))
+
+        def load_list(name, src):
+            tile = lists.tile(list(src.shape), U16, name=name)
+            nc.sync.dma_start(tile[:], src)
+            return tile
+
+        def load_dealt(queue, name, src):
+            tile = keep.tile([P, PACK], F32, name=name)
+            queue.dma_start(out=tile[:], in_=src.rearrange("(p t) o -> p (t o)", t=PACK))
+            return tile
+
+        ta_rows = ta.rearrange("(p t) c -> p t c", t=PACK)
+
+        def load_table(t):
+            tile = keep.tile([P, T], F32, name="table%d" % t)
+            nc.sync.dma_start(out=tile[:], in_=ta_rows[:, t, :])
+            return tile
+
+        def load_words(name, src, dtype, width):
+            tile = keep.tile([P, width], dtype, name=name, align_bytes=64)
+            nc.sync.dma_start(out=tile[:].bitcast(I32), in_=src.bitcast(I32))
+            return tile
+
+        def stage_scales(stage, first, src):
+            rows = src[0].bitcast(I32).rearrange("(q i) n -> i q n", i=4)
+            nc.sync.dma_start(out=stage[:, :, first : first + rows.shape[2]], in_=rows)
+
+        def spread_scales(plane, stage):
+            for q in range(QUADS):
+                nc.vector.tensor_copy(out=plane[32 * q : 32 * q + 4, :].bitcast(I32), in_=stage[:, q, :])
+
+        def bank():
+            return psum.tile([P, BANK], F32, name="bank")
+
+        idx = load_list("idx", offs)
+        ga_sb = load_dealt(nc.scalar, "ga_sb", ga)
+        tables = [load_table(0)]
+        gb_sb = load_dealt(nc.scalar, "gb_sb", gb)
+        idx2 = load_list("idx2", offs2)
+        xo_stage = keep.tile([4, QUADS, M // 4], I32, name="xo_stage")
+        stage_scales(xo_stage, 0, xo_scales)
+        idx3 = load_list("idx3", offs3)
+        w2_stage = keep.tile([4, QUADS, R // 4], I32, name="w2_stage")
+        stage_scales(w2_stage, 0, w2_scales)
+        w2_raw = load_words("w2_raw", w2_words[0], U8, 2 * R)
+        xo_sb = load_words("xo_sb", xo_words[0].rearrange("p n t -> p (n t)"), U32, M)
+        tables.append(load_table(1))
+        w_stage = keep.tile([4, QUADS, (R + N) // 4], I32, name="w_stage")
+        stage_scales(w_stage, 0, w_scales)
+        stage_scales(w_stage, R // 4, wb_scales)
+        tables.extend(load_table(t) for t in (2, 3))
+        w_raw = load_words("w_raw", w_words[0].rearrange("p n t -> p (n t)"), U32, R)
+        idx5 = load_list("idx5", offs5)
+        sb_sb = load_dealt(nc.sync, "sb_sb", sb)
+        idx4 = load_list("idx4", offs4)
+        sa_sb = load_dealt(nc.sync, "sa_sb", sa)
+        wb_sb = load_words("wb_sb", wb_words[0], U8, 2 * N)
+        so_sb = keep.tile([P, N // P, 1], F32, name="so_sb")
+        with nc.allow_non_contiguous_dma(reason="one value a partition for each block of 128 output features"):
+            nc.sync.dma_start(out=so_sb[:], in_=so.rearrange("(c p) o -> p c o", p=P))
+        idx6 = load_list("idx6", offs6)
+        idx7 = load_list("idx7", offs7)
+
+        def cleared_plane(name, width):
+            plane = keep.tile([P, width], U8, name=name, align_bytes=64)
+            nc.vector.memset(plane[:].bitcast(I32), 0)
+            return plane
+
+        def deal_scales(name, plane):
+            dealt = keep.tile([P, R], U8, name=name, align_bytes=64)
+            nc.vector.tensor_copy(
+                out=dealt[:].rearrange("p (t m) -> p m t", t=PACK),
+                in_=plane[:, 0:R].rearrange("p (m t) -> p m t", t=PACK),
+            )
+            return dealt
+
+        xo_plane = cleared_plane("xo_plane", M)
+        w2_plane = cleared_plane("w2_plane", R)
+        w_plane = cleared_plane("w_plane", R + N)
+        pages = []
+        for c in range(N // P):
+            page = keep.tile([P, E], F32, name="page%d" % c)
+            nc.vector.memset(page[:], 0.0)
+            pages.append(page)
+        spread_scales(xo_plane, xo_stage)
+        spread_scales(w2_plane, w2_stage)
+        note_scales = keep.tile([P, J], U8, name="note_scales", align_bytes=64)
+        nc.vector.tensor_copy(out=note_scales[:], in_=xo_plane[:].indirect(idx3[:]))
+        w2_dealt_scales = deal_scales("w2_dealt_scales", w2_plane)
+        note_codes = keep.tile([P, J], U32, name="note_codes", align_bytes=64)
+        nc.vector.tensor_copy(out=note_codes[:], in_=xo_sb[:].indirect(idx3[:]))
+
+        coarse, fine = [], []
+
+        def look_up(t):
+            g1 = keep.tile([P, J], F32, name="coarse%d" % t)
+            nc.scalar.activation(out=g1[:], in_=tables[t][:].indirect(idx[:]), func=COPY, scale=ga_sb[:, t : t + 1])
+            g2 = keep.tile([P, J], F32, name="fine%d" % t)
+            nc.scalar.activation(out=g2[:], in_=tables[t][:].indirect(idx2[:]), func=COPY, scale=gb_sb[:, t : t + 1])
+            coarse.append(g1)
+            fine.append(g2)
+
+        xc_early = keep.tile([P, PACK - 1, J], BF16, name="xc_early")
+
+        def add_plane(t):
+            nc.vector.tensor_tensor(out=xc_early[:, t, :], in0=coarse[t][:], in1=fine[t][:], op=ADD)
+
+        look_up(0)
+        w2_dealt = keep.tile([P, 2 * R], U8, name="w2_dealt", align_bytes=64)
+        nc.scalar.copy(
+            out=w2_dealt[:].bitcast(U16).rearrange("p (t m) -> p m t", t=PACK),
+            in_=w2_raw[:].bitcast(U16).rearrange("p (m t) -> p m t", t=PACK),
+        )
+        add_plane(0)
+
+        b_rows = []
+        for t in range(PACK):
+            acc = bank()
+            nc.tensor.matmul_mx(
+                out=acc[:],
+                lhsT=w2_dealt[:, 2 * P * t : 2 * P * (t + 1)].bitcast(FP4X4),
+                lhsT_scale=w2_dealt_scales[:, P * t : P * (t + 1)],
+                rhs=note_codes[:].bitcast(FP8X4),
+                rhs_scale=note_scales[:],
+                start=True,
+                stop=True,
+            )
+            rows = keep.tile([P, J], F32, name="b_rows%d" % t)
+            nc.vector.tensor_copy(out=rows[:], in_=acc[:])
+            b_rows.append(rows)
+
+        spread_scales(w_plane, w_stage)
+        w_dealt_scales = deal_scales("w_dealt_scales", w_plane)
+        for t in (1, 2):
+            look_up(t)
+            add_plane(t)
+        HJ = J // 2
+        woven = []
+        for h in range(2):
+            tile = keep.tile([P, HJ, PACK], BF16, name="woven%d" % h, align_bytes=64)
+            nc.vector.tensor_copy(
+                out=tile[:, :, 0 : PACK - 1],
+                in_=xc_early[:, :, HJ * h : HJ * (h + 1)].rearrange("p t j -> p j t"),
+            )
+            woven.append(tile)
+        w_dealt = keep.tile([P, R], U32, name="w_dealt", align_bytes=64)
+        nc.vector.tensor_copy(
+            out=w_dealt[:].bitcast(I32).rearrange("p (t m) -> p m t", t=PACK),
+            in_=w_raw[:].bitcast(I32).rearrange("p (m t) -> p m t", t=PACK),
+        )
+        look_up(3)
+
+        b_picked = keep.tile([P, PACK, O], F32, name="b_picked", tag="table3")
+        for t in range(PACK):
+            nc.scalar.activation(
+                out=b_picked[:, t, :], in_=b_rows[t][:].indirect(idx5[:]), func=COPY, scale=sb_sb[:, t : t + 1]
+            )
+
+        xc_last = []
+        for h in range(2):
+            cols = slice(HJ * h, HJ * (h + 1))
+            tile = keep.tile([P, HJ], BF16, name="xc_last%d" % h)
+            nc.vector.tensor_tensor(out=tile[:], in0=coarse[3][:, cols], in1=fine[3][:, cols], op=ADD)
+            xc_last.append(tile)
+        for h in range(2):
+            nc.vector.tensor_copy(out=woven[h][:, :, PACK - 1], in_=xc_last[h][:])
+        xc_codes = keep.tile([P, J], U32, name="xc_codes", align_bytes=64)
+        xc_scales = keep.tile([P, J], U8, name="xc_scales", align_bytes=64)
+        for h in range(2):
+            cols = slice(HJ * h, HJ * (h + 1))
+            nc.vector.quantize_mx(
+                out=xc_codes[:, cols].bitcast(FP8X4),
+                scales=xc_scales[:, cols],
+                in_=woven[h][:].rearrange("p j t -> p (j t)"),
+            )
+
+        a_rows = []
+        for t in range(PACK):
+            rows = keep.tile([P, J], F32, name="a_rows%d" % t)
+            pieces = [slice(0, HJ), slice(HJ, J)] if t == 0 else [slice(0, J)]
+            for cols in pieces:
+                acc = bank()
+                nc.tensor.matmul_mx(
+                    out=acc[:, cols],
+                    lhsT=w_dealt[:, P * t : P * (t + 1)].bitcast(FP8X4),
+                    lhsT_scale=w_dealt_scales[:, P * t : P * (t + 1)],
+                    rhs=xc_codes[:, cols].bitcast(FP8X4),
+                    rhs_scale=xc_scales[:, cols],
+                    start=True,
+                    stop=True,
+                )
+                nc.vector.tensor_copy(out=rows[:, cols], in_=acc[:, cols])
+            a_rows.append(rows)
+
+        HO = O // 2
+        a_low = keep.tile([P, 2, O], F32, name="a_low")
+        for t in range(2):
+            nc.scalar.activation(
+                out=a_low[:, t, :], in_=a_rows[t][:].indirect(idx4[:]), func=COPY, scale=sa_sb[:, t : t + 1]
+            )
+        a_high = []
+        for h in range(2):
+            tile = keep.tile([P, 2, HO], F32, name="a_high%d" % h)
+            for t in (2, 3):
+                nc.scalar.activation(
+                    out=tile[:, t - 2, :],
+                    in_=a_rows[t][:].indirect(idx4[:, HO // 16 * h : HO // 16 * (h + 1)]),
+                    func=COPY,
+                    scale=sa_sb[:, t : t + 1],
+                )
+            a_high.append(tile)
+
+        hid = []
+        for h in range(2):
+            cols = slice(HO * h, HO * (h + 1))
+            tile = keep.tile([P, HO, PACK], BF16, name="hid%d" % h, align_bytes=64)
+            nc.vector.tensor_tensor(
+                out=tile[:, :, 0:2],
+                in0=a_low[:, :, cols].rearrange("p t o -> p o t"),
+                in1=b_picked[:, 0:2, cols].rearrange("p t o -> p o t"),
+                op=MAX,
+            )
+            hid.append(tile)
+        for h in range(2):
+            cols = slice(HO * h, HO * (h + 1))
+            nc.vector.tensor_tensor(
+                out=hid[h][:, :, 2:4],
+                in0=a_high[h][:].rearrange("p t o -> p o t"),
+                in1=b_picked[:, 2:4, cols].rearrange("p t o -> p o t"),
+                op=MAX,
+            )
+        p_rows = [keep.tile([P, O], F32, name="p_rows%d" % c) for c in range(N // P)]
+        p_banks = []
+        for h in range(2):
+            codes = keep.tile([P, HO], U32, name="hid_codes%d" % h, align_bytes=64)
+            scales = keep.tile([P, HO], U8, name="hid_scales%d" % h, align_bytes=64)
+            nc.vector.quantize_mx(
+                out=codes[:].bitcast(FP8X4), scales=scales[:], in_=hid[h][:].rearrange("p o t -> p (o t)")
+            )
+            for c in range(N // P):
+                acc = bank()
+                nc.tensor.matmul_mx(
+                    out=acc[:, 0:HO],
+                    lhsT=wb_sb[:, 2 * P * c : 2 * P * (c + 1)].bitcast(FP4X4),
+                    lhsT_scale=w_plane[:, R + P * c : R + P * (c + 1)],
+                    rhs=codes[:].bitcast(FP8X4),
+                    rhs_scale=scales[:],
+                    start=True,
+                    stop=True,
+                )
+                p_banks.append(acc)
+        for h in range(2):
+            cols = slice(HO * h, HO * (h + 1))
+            nc.scalar.copy(out=p_rows[0][:, cols], in_=p_banks[2 * h][:, 0:HO])
+            nc.vector.tensor_copy(out=p_rows[1][:, cols], in_=p_banks[2 * h + 1][:, 0:HO])
+        for c in range(N // P):
+            ends = keep.tile([P, U], F32, name="ends%d" % c)
+            nc.scalar.activation(out=ends[:], in_=p_rows[c][:].indirect(idx6[:]), func=COPY, scale=so_sb[:, c, :])
+            nc.vector.tensor_copy(out=pages[c][:].indirect(idx7[:]), in_=ends[:])
+            nc.sync.dma_start(out=out[P * c : P * (c + 1), :], in_=pages[c][:])

@@ -66,23 +66,21 @@ def tile_picked_refined_plain_two_groupmeet_one_posted_kernel(
         def bank():
             return psum.tile([P, BANK], F32, name="bank")
 
-        idx = load_list("idx", offs)
+        w2_raw = load_words("w2_raw", w2_words[0], U8, 2 * R)
         ga_sb = load_dealt(nc.scalar, "ga_sb", ga)
-        tables = [load_table(0)]
+        idx = load_list("idx", offs)
         gb_sb = load_dealt(nc.scalar, "gb_sb", gb)
         idx2 = load_list("idx2", offs2)
+        idx3 = load_list("idx3", offs3)
+        tables = [load_table(0)]
         xo_stage = keep.tile([4, QUADS, M // 4], I32, name="xo_stage")
         stage_scales(xo_stage, 0, xo_scales)
-        idx3 = load_list("idx3", offs3)
-        w2_stage = keep.tile([4, QUADS, R // 4], I32, name="w2_stage")
-        stage_scales(w2_stage, 0, w2_scales)
-        w2_raw = load_words("w2_raw", w2_words[0], U8, 2 * R)
+        w_stage = keep.tile([4, QUADS, (R + R + N) // 4], I32, name="w_stage")
+        stage_scales(w_stage, 0, w2_scales)
+        stage_scales(w_stage, R // 4, w_scales)
+        stage_scales(w_stage, 2 * R // 4, wb_scales)
         xo_sb = load_words("xo_sb", xo_words[0].rearrange("p n t -> p (n t)"), U32, M)
-        tables.append(load_table(1))
-        w_stage = keep.tile([4, QUADS, (R + N) // 4], I32, name="w_stage")
-        stage_scales(w_stage, 0, w_scales)
-        stage_scales(w_stage, R // 4, wb_scales)
-        tables.extend(load_table(t) for t in (2, 3))
+        tables.extend(load_table(t) for t in range(1, PACK))
         w_raw = load_words("w_raw", w_words[0].rearrange("p n t -> p (n t)"), U32, R)
         idx5 = load_list("idx5", offs5)
         sb_sb = load_dealt(nc.sync, "sb_sb", sb)
@@ -100,27 +98,22 @@ def tile_picked_refined_plain_two_groupmeet_one_posted_kernel(
             nc.vector.memset(plane[:].bitcast(I32), 0)
             return plane
 
-        def deal_scales(name, plane):
-            dealt = keep.tile([P, R], U8, name=name, align_bytes=64)
-            nc.vector.tensor_copy(
-                out=dealt[:].rearrange("p (t m) -> p m t", t=PACK),
-                in_=plane[:, 0:R].rearrange("p (m t) -> p m t", t=PACK),
-            )
-            return dealt
-
         xo_plane = cleared_plane("xo_plane", M)
-        w2_plane = cleared_plane("w2_plane", R)
-        w_plane = cleared_plane("w_plane", R + N)
+        w_plane = cleared_plane("w_plane", R + R + N)
         pages = []
         for c in range(N // P):
             page = keep.tile([P, E], F32, name="page%d" % c)
             nc.vector.memset(page[:], 0.0)
             pages.append(page)
         spread_scales(xo_plane, xo_stage)
-        spread_scales(w2_plane, w2_stage)
         note_scales = keep.tile([P, J], U8, name="note_scales", align_bytes=64)
         nc.vector.tensor_copy(out=note_scales[:], in_=xo_plane[:].indirect(idx3[:]))
-        w2_dealt_scales = deal_scales("w2_dealt_scales", w2_plane)
+        spread_scales(w_plane, w_stage)
+        dealt_scales = keep.tile([P, 2, R], U8, name="dealt_scales", align_bytes=64)
+        nc.vector.tensor_copy(
+            out=dealt_scales[:].rearrange("p s (t m) -> p s m t", t=PACK),
+            in_=w_plane[:, 0 : 2 * R].rearrange("p (s m t) -> p s m t", s=2, t=PACK),
+        )
         note_codes = keep.tile([P, J], U32, name="note_codes", align_bytes=64)
         nc.vector.tensor_copy(out=note_codes[:], in_=xo_sb[:].indirect(idx3[:]))
 
@@ -129,23 +122,16 @@ def tile_picked_refined_plain_two_groupmeet_one_posted_kernel(
         def look_up(t):
             g1 = keep.tile([P, J], F32, name="coarse%d" % t)
             nc.scalar.activation(out=g1[:], in_=tables[t][:].indirect(idx[:]), func=COPY, scale=ga_sb[:, t : t + 1])
-            g2 = keep.tile([P, J], F32, name="fine%d" % t)
+            g2 = keep.tile([P, J], F32, name="fine%d" % t, align_bytes=64)
             nc.scalar.activation(out=g2[:], in_=tables[t][:].indirect(idx2[:]), func=COPY, scale=gb_sb[:, t : t + 1])
             coarse.append(g1)
             fine.append(g2)
 
-        xc_early = keep.tile([P, PACK - 1, J], BF16, name="xc_early")
-
-        def add_plane(t):
-            nc.vector.tensor_tensor(out=xc_early[:, t, :], in0=coarse[t][:], in1=fine[t][:], op=ADD)
-
-        look_up(0)
-        w2_dealt = keep.tile([P, 2 * R], U8, name="w2_dealt", align_bytes=64)
+        w2_dealt = keep.tile([P, 2 * R], U8, name="w2_dealt", tag="relay", align_bytes=64)
         nc.scalar.copy(
             out=w2_dealt[:].bitcast(U16).rearrange("p (t m) -> p m t", t=PACK),
             in_=w2_raw[:].bitcast(U16).rearrange("p (m t) -> p m t", t=PACK),
         )
-        add_plane(0)
 
         b_rows = []
         for t in range(PACK):
@@ -153,7 +139,7 @@ def tile_picked_refined_plain_two_groupmeet_one_posted_kernel(
             nc.tensor.matmul_mx(
                 out=acc[:],
                 lhsT=w2_dealt[:, 2 * P * t : 2 * P * (t + 1)].bitcast(FP4X4),
-                lhsT_scale=w2_dealt_scales[:, P * t : P * (t + 1)],
+                lhsT_scale=dealt_scales[:, 0, P * t : P * (t + 1)],
                 rhs=note_codes[:].bitcast(FP8X4),
                 rhs_scale=note_scales[:],
                 start=True,
@@ -163,21 +149,30 @@ def tile_picked_refined_plain_two_groupmeet_one_posted_kernel(
             nc.vector.tensor_copy(out=rows[:], in_=acc[:])
             b_rows.append(rows)
 
-        spread_scales(w_plane, w_stage)
-        w_dealt_scales = deal_scales("w_dealt_scales", w_plane)
-        for t in (1, 2):
-            look_up(t)
-            add_plane(t)
         HJ = J // 2
+        xc_low = keep.tile([P, 2, J], BF16, name="xc_low", tag="relay", align_bytes=64)
+        for t in (0, 1):
+            look_up(t)
+            nc.vector.tensor_tensor(out=xc_low[:, t, :], in0=coarse[t][:], in1=fine[t][:], op=ADD)
         woven = []
         for h in range(2):
             tile = keep.tile([P, HJ, PACK], BF16, name="woven%d" % h, align_bytes=64)
             nc.vector.tensor_copy(
-                out=tile[:, :, 0 : PACK - 1],
-                in_=xc_early[:, :, HJ * h : HJ * (h + 1)].rearrange("p t j -> p j t"),
+                out=tile[:, :, 0:2], in_=xc_low[:, :, HJ * h : HJ * (h + 1)].rearrange("p t j -> p j t")
             )
             woven.append(tile)
-        w_dealt = keep.tile([P, R], U32, name="w_dealt", align_bytes=64)
+        xc_high = [keep.tile([P, 2, HJ], BF16, name="xc_high%d" % h) for h in range(2)]
+
+        def add_high(t):
+            for h in range(2):
+                cols = slice(HJ * h, HJ * (h + 1))
+                nc.vector.tensor_tensor(
+                    out=xc_high[h][:, t - 2, :], in0=coarse[t][:, cols], in1=fine[t][:, cols], op=ADD
+                )
+
+        look_up(2)
+        add_high(2)
+        w_dealt = keep.tile([P, R], U32, name="w_dealt", tag="fine2", align_bytes=64)
         nc.vector.tensor_copy(
             out=w_dealt[:].bitcast(I32).rearrange("p (t m) -> p m t", t=PACK),
             in_=w_raw[:].bitcast(I32).rearrange("p (m t) -> p m t", t=PACK),
@@ -190,14 +185,9 @@ def tile_picked_refined_plain_two_groupmeet_one_posted_kernel(
                 out=b_picked[:, t, :], in_=b_rows[t][:].indirect(idx5[:]), func=COPY, scale=sb_sb[:, t : t + 1]
             )
 
-        xc_last = []
+        add_high(3)
         for h in range(2):
-            cols = slice(HJ * h, HJ * (h + 1))
-            tile = keep.tile([P, HJ], BF16, name="xc_last%d" % h)
-            nc.vector.tensor_tensor(out=tile[:], in0=coarse[3][:, cols], in1=fine[3][:, cols], op=ADD)
-            xc_last.append(tile)
-        for h in range(2):
-            nc.vector.tensor_copy(out=woven[h][:, :, PACK - 1], in_=xc_last[h][:])
+            nc.vector.tensor_copy(out=woven[h][:, :, 2:4], in_=xc_high[h][:].rearrange("p t j -> p j t"))
         xc_codes = keep.tile([P, J], U32, name="xc_codes", align_bytes=64)
         xc_scales = keep.tile([P, J], U8, name="xc_scales", align_bytes=64)
         for h in range(2):
@@ -217,7 +207,7 @@ def tile_picked_refined_plain_two_groupmeet_one_posted_kernel(
                 nc.tensor.matmul_mx(
                     out=acc[:, cols],
                     lhsT=w_dealt[:, P * t : P * (t + 1)].bitcast(FP8X4),
-                    lhsT_scale=w_dealt_scales[:, P * t : P * (t + 1)],
+                    lhsT_scale=dealt_scales[:, 1, P * t : P * (t + 1)],
                     rhs=xc_codes[:, cols].bitcast(FP8X4),
                     rhs_scale=xc_scales[:, cols],
                     start=True,
@@ -232,22 +222,20 @@ def tile_picked_refined_plain_two_groupmeet_one_posted_kernel(
             nc.scalar.activation(
                 out=a_low[:, t, :], in_=a_rows[t][:].indirect(idx4[:]), func=COPY, scale=sa_sb[:, t : t + 1]
             )
-        a_high = []
-        for h in range(2):
-            tile = keep.tile([P, 2, HO], F32, name="a_high%d" % h)
-            for t in (2, 3):
+        a_high = [keep.tile([P, 2, HO], F32, name="a_high%d" % h) for h in range(2)]
+        for t in (2, 3):
+            for h in range(2):
                 nc.scalar.activation(
-                    out=tile[:, t - 2, :],
+                    out=a_high[h][:, t - 2, :],
                     in_=a_rows[t][:].indirect(idx4[:, HO // 16 * h : HO // 16 * (h + 1)]),
                     func=COPY,
                     scale=sa_sb[:, t : t + 1],
                 )
-            a_high.append(tile)
 
         hid = []
         for h in range(2):
             cols = slice(HO * h, HO * (h + 1))
-            tile = keep.tile([P, HO, PACK], BF16, name="hid%d" % h, align_bytes=64)
+            tile = keep.tile([P, HO, PACK], BF16, name="hid%d" % h, tag=("xc_codes", "fine2")[h], align_bytes=64)
             nc.vector.tensor_tensor(
                 out=tile[:, :, 0:2],
                 in0=a_low[:, :, cols].rearrange("p t o -> p o t"),
@@ -276,17 +264,17 @@ def tile_picked_refined_plain_two_groupmeet_one_posted_kernel(
                 nc.tensor.matmul_mx(
                     out=acc[:, 0:HO],
                     lhsT=wb_sb[:, 2 * P * c : 2 * P * (c + 1)].bitcast(FP4X4),
-                    lhsT_scale=w_plane[:, R + P * c : R + P * (c + 1)],
+                    lhsT_scale=w_plane[:, 2 * R + P * c : 2 * R + P * (c + 1)],
                     rhs=codes[:].bitcast(FP8X4),
                     rhs_scale=scales[:],
                     start=True,
                     stop=True,
                 )
                 p_banks.append(acc)
-        for h in range(2):
-            cols = slice(HO * h, HO * (h + 1))
-            nc.scalar.copy(out=p_rows[0][:, cols], in_=p_banks[2 * h][:, 0:HO])
-            nc.vector.tensor_copy(out=p_rows[1][:, cols], in_=p_banks[2 * h + 1][:, 0:HO])
+        for c in range(N // P):
+            nc.scalar.copy(out=p_rows[c][:, 0:HO], in_=p_banks[c][:, 0:HO])
+        for c in range(N // P):
+            nc.vector.tensor_copy(out=p_rows[c][:, HO:O], in_=p_banks[2 + c][:, 0:HO])
         for c in range(N // P):
             ends = keep.tile([P, U], F32, name="ends%d" % c)
             nc.scalar.activation(out=ends[:], in_=p_rows[c][:].indirect(idx6[:]), func=COPY, scale=so_sb[:, c, :])

@@ -31,6 +31,7 @@ def tile_picked_refined_plain_two_groupmeet_one_posted_kernel(
     with ExitStack() as ctx:
         lists = ctx.enter_context(tc.tile_pool(name="lists", bufs=1))
         keep = ctx.enter_context(tc.tile_pool(name="keep", bufs=1))
+        last = ctx.enter_context(tc.tile_pool(name="last", bufs=1))
         psum = ctx.enter_context(tc.psum_pool(name="psum", bufs=8))
 
         def load_list(name, src):
@@ -46,7 +47,10 @@ def tile_picked_refined_plain_two_groupmeet_one_posted_kernel(
         ta_rows = ta.rearrange("(p t) c -> p t c", t=PACK)
 
         def load_table(t):
-            tile = keep.tile([P, T], F32, name="table%d" % t)
+            if t == PACK - 1:
+                tile = last.tile([P, T], F32, name="table%d" % t, offset=0)
+            else:
+                tile = keep.tile([P, T], F32, name="table%d" % t)
             nc.sync.dma_start(out=tile[:], in_=ta_rows[:, t, :])
             return tile
 
@@ -55,32 +59,40 @@ def tile_picked_refined_plain_two_groupmeet_one_posted_kernel(
             nc.sync.dma_start(out=tile[:].bitcast(I32), in_=src.bitcast(I32))
             return tile
 
-        def stage_scales(stage, first, src):
-            rows = src[0].bitcast(I32).rearrange("(q i) n -> i q n", i=4)
-            nc.sync.dma_start(out=stage[:, :, first : first + rows.shape[2]], in_=rows)
+        def stage_scales(queues, stage, first, src):
+            halves = len(queues)
+            rows = src[0].bitcast(I32).rearrange("(u q i) n -> u i q n", u=halves, i=4)
+            for u in range(halves):
+                queues[u].dma_start(out=stage[64 * u : 64 * u + 4, :, first : first + rows.shape[3]], in_=rows[u])
 
         def spread_scales(plane, stage):
+            held = stage.shape[1]
             for q in range(QUADS):
-                nc.vector.tensor_copy(out=plane[32 * q : 32 * q + 4, :].bitcast(I32), in_=stage[:, q, :])
+                first = 64 * (q // held)
+                nc.vector.tensor_copy(
+                    out=plane[32 * q : 32 * q + 4, :].bitcast(I32), in_=stage[first : first + 4, q % held, :]
+                )
 
         def bank():
             return psum.tile([P, BANK], F32, name="bank")
 
-        w2_raw = load_words("w2_raw", w2_words[0], U8, 2 * R)
+        xo_stage = keep.tile([P, 2, M // 4], I32, name="xo_stage")
+        stage_scales((nc.scalar, nc.scalar), xo_stage, 0, xo_scales)
         ga_sb = load_dealt(nc.scalar, "ga_sb", ga)
-        idx = load_list("idx", offs)
         gb_sb = load_dealt(nc.scalar, "gb_sb", gb)
-        idx2 = load_list("idx2", offs2)
+        w2_raw = load_words("w2_raw", w2_words[0], U8, 2 * R)
         idx3 = load_list("idx3", offs3)
+        idx = load_list("idx", offs)
         tables = [load_table(0)]
-        xo_stage = keep.tile([4, QUADS, M // 4], I32, name="xo_stage")
-        stage_scales(xo_stage, 0, xo_scales)
-        w_stage = keep.tile([4, QUADS, (R + R + N) // 4], I32, name="w_stage")
-        stage_scales(w_stage, 0, w2_scales)
-        stage_scales(w_stage, R // 4, w_scales)
-        stage_scales(w_stage, 2 * R // 4, wb_scales)
+        idx2 = load_list("idx2", offs2)
+        w_stage = keep.tile([P, 2, 2 * R // 4], I32, name="w_stage")
+        stage_scales((nc.sync, nc.sync), w_stage, 0, w2_scales)
+        stage_scales((nc.sync, nc.sync), w_stage, R // 4, w_scales)
+        tables.append(load_table(1))
+        wb_stage = keep.tile([P, QUADS, N // 4], I32, name="wb_stage", align_bytes=64)
+        stage_scales((nc.sync,), wb_stage, 0, wb_scales)
+        tables.extend(load_table(t) for t in (2, 3))
         xo_sb = load_words("xo_sb", xo_words[0].rearrange("p n t -> p (n t)"), U32, M)
-        tables.extend(load_table(t) for t in range(1, PACK))
         w_raw = load_words("w_raw", w_words[0].rearrange("p n t -> p (n t)"), U32, R)
         idx5 = load_list("idx5", offs5)
         sb_sb = load_dealt(nc.sync, "sb_sb", sb)
@@ -93,13 +105,13 @@ def tile_picked_refined_plain_two_groupmeet_one_posted_kernel(
         idx6 = load_list("idx6", offs6)
         idx7 = load_list("idx7", offs7)
 
-        def cleared_plane(name, width):
-            plane = keep.tile([P, width], U8, name=name, align_bytes=64)
+        def cleared_plane(name, width, tag):
+            plane = keep.tile([P, width], U8, name=name, tag=tag, align_bytes=64)
             nc.vector.memset(plane[:].bitcast(I32), 0)
             return plane
 
-        xo_plane = cleared_plane("xo_plane", M)
-        w_plane = cleared_plane("w_plane", R + R + N)
+        xo_plane = cleared_plane("xo_plane", M, "xo_plane")
+        w_plane = cleared_plane("w_plane", 2 * R, "w_plane")
         pages = []
         for c in range(N // P):
             page = keep.tile([P, E], F32, name="page%d" % c)
@@ -112,42 +124,24 @@ def tile_picked_refined_plain_two_groupmeet_one_posted_kernel(
         dealt_scales = keep.tile([P, 2, R], U8, name="dealt_scales", align_bytes=64)
         nc.vector.tensor_copy(
             out=dealt_scales[:].rearrange("p s (t m) -> p s m t", t=PACK),
-            in_=w_plane[:, 0 : 2 * R].rearrange("p (s m t) -> p s m t", s=2, t=PACK),
+            in_=w_plane[:].rearrange("p (s m t) -> p s m t", s=2, t=PACK),
         )
-        note_codes = keep.tile([P, J], U32, name="note_codes", align_bytes=64)
-        nc.vector.tensor_copy(out=note_codes[:], in_=xo_sb[:].indirect(idx3[:]))
 
         coarse, fine = [], []
 
         def look_up(t):
-            g1 = keep.tile([P, J], F32, name="coarse%d" % t)
+            g1 = keep.tile([P, J], F32, name="coarse%d" % t, align_bytes=64)
             nc.scalar.activation(out=g1[:], in_=tables[t][:].indirect(idx[:]), func=COPY, scale=ga_sb[:, t : t + 1])
             g2 = keep.tile([P, J], F32, name="fine%d" % t, align_bytes=64)
             nc.scalar.activation(out=g2[:], in_=tables[t][:].indirect(idx2[:]), func=COPY, scale=gb_sb[:, t : t + 1])
             coarse.append(g1)
             fine.append(g2)
 
-        w2_dealt = keep.tile([P, 2 * R], U8, name="w2_dealt", tag="relay", align_bytes=64)
+        w2_dealt = keep.tile([P, 2 * R], U8, name="w2_dealt", tag="w2_dealt", align_bytes=64)
         nc.scalar.copy(
             out=w2_dealt[:].bitcast(U16).rearrange("p (t m) -> p m t", t=PACK),
             in_=w2_raw[:].bitcast(U16).rearrange("p (m t) -> p m t", t=PACK),
         )
-
-        b_rows = []
-        for t in range(PACK):
-            acc = bank()
-            nc.tensor.matmul_mx(
-                out=acc[:],
-                lhsT=w2_dealt[:, 2 * P * t : 2 * P * (t + 1)].bitcast(FP4X4),
-                lhsT_scale=dealt_scales[:, 0, P * t : P * (t + 1)],
-                rhs=note_codes[:].bitcast(FP8X4),
-                rhs_scale=note_scales[:],
-                start=True,
-                stop=True,
-            )
-            rows = keep.tile([P, J], F32, name="b_rows%d" % t)
-            nc.vector.tensor_copy(out=rows[:], in_=acc[:])
-            b_rows.append(rows)
 
         HJ = J // 2
         xc_low = keep.tile([P, 2, J], BF16, name="xc_low", tag="relay", align_bytes=64)
@@ -161,33 +155,61 @@ def tile_picked_refined_plain_two_groupmeet_one_posted_kernel(
                 out=tile[:, :, 0:2], in_=xc_low[:, :, HJ * h : HJ * (h + 1)].rearrange("p t j -> p j t")
             )
             woven.append(tile)
-        xc_high = [keep.tile([P, 2, HJ], BF16, name="xc_high%d" % h) for h in range(2)]
-
-        def add_high(t):
-            for h in range(2):
-                cols = slice(HJ * h, HJ * (h + 1))
-                nc.vector.tensor_tensor(
-                    out=xc_high[h][:, t - 2, :], in0=coarse[t][:, cols], in1=fine[t][:, cols], op=ADD
-                )
-
         look_up(2)
-        add_high(2)
-        w_dealt = keep.tile([P, R], U32, name="w_dealt", tag="fine2", align_bytes=64)
-        nc.vector.tensor_copy(
-            out=w_dealt[:].bitcast(I32).rearrange("p (t m) -> p m t", t=PACK),
-            in_=w_raw[:].bitcast(I32).rearrange("p (m t) -> p m t", t=PACK),
-        )
+        wb_plane = cleared_plane("wb_plane", N, "relay")
+        spread_scales(wb_plane, wb_stage)
+        xc_high = keep.tile([P, 2, J], BF16, name="xc_high")
+        nc.vector.tensor_tensor(out=xc_high[:, 0, :], in0=coarse[2][:], in1=fine[2][:], op=ADD)
+        note_codes = keep.tile([P, J], U32, name="note_codes", tag="fine2", align_bytes=64)
+        for h in range(2):
+            nc.vector.tensor_copy(
+                out=note_codes[:, HJ * h : HJ * (h + 1)],
+                in_=xo_sb[:].indirect(idx3[:, HJ // 16 * h : HJ // 16 * (h + 1)]),
+            )
         look_up(3)
+        w_dealt = last.tile([P, R], U32, name="w_dealt", offset=0, align_bytes=64)
+        nc.scalar.copy(
+            out=w_dealt[:].rearrange("p (t m) -> p m t", t=PACK),
+            in_=w_raw[:].rearrange("p (m t) -> p m t", t=PACK),
+        )
 
-        b_picked = keep.tile([P, PACK, O], F32, name="b_picked", tag="table3")
-        for t in range(PACK):
-            nc.scalar.activation(
-                out=b_picked[:, t, :], in_=b_rows[t][:].indirect(idx5[:]), func=COPY, scale=sb_sb[:, t : t + 1]
+        b_banks = [bank() for t in range(PACK)]
+
+        def b_product(t, cols):
+            nc.tensor.matmul_mx(
+                out=b_banks[t][:, cols],
+                lhsT=w2_dealt[:, 2 * P * t : 2 * P * (t + 1)].bitcast(FP4X4),
+                lhsT_scale=dealt_scales[:, 0, P * t : P * (t + 1)],
+                rhs=note_codes[:, cols].bitcast(FP8X4),
+                rhs_scale=note_scales[:, cols],
+                start=True,
+                stop=True,
             )
 
-        add_high(3)
         for h in range(2):
-            nc.vector.tensor_copy(out=woven[h][:, :, 2:4], in_=xc_high[h][:].rearrange("p t j -> p j t"))
+            for t in (0, 1):
+                b_product(t, slice(HJ * h, HJ * (h + 1)))
+        for t in (2, 3):
+            b_product(t, slice(0, J))
+        b_picked = keep.tile([P, PACK, O], F32, name="b_picked")
+
+        def pick_b(t, rows):
+            nc.scalar.activation(
+                out=b_picked[:, t, :], in_=rows[:].indirect(idx5[:]), func=COPY, scale=sb_sb[:, t : t + 1]
+            )
+
+        b_low = [last.tile([P, J], F32, name="b_rows%d" % t, offset=4 * (R + J * t)) for t in (0, 1)]
+        for t in (0, 1):
+            nc.scalar.copy(out=b_low[t][:], in_=b_banks[t][:])
+        for t in (0, 1):
+            pick_b(t, b_low[t])
+
+        for h in range(2):
+            cols = slice(HJ * h, HJ * (h + 1))
+            nc.vector.tensor_tensor(out=xc_high[:, 1, cols], in0=coarse[3][:, cols], in1=fine[3][:, cols], op=ADD)
+        for h in range(2):
+            cols = slice(HJ * h, HJ * (h + 1))
+            nc.vector.tensor_copy(out=woven[h][:, :, 2:4], in_=xc_high[:, :, cols].rearrange("p t j -> p j t"))
         xc_codes = keep.tile([P, J], U32, name="xc_codes", align_bytes=64)
         xc_scales = keep.tile([P, J], U8, name="xc_scales", align_bytes=64)
         for h in range(2):
@@ -198,12 +220,11 @@ def tile_picked_refined_plain_two_groupmeet_one_posted_kernel(
                 in_=woven[h][:].rearrange("p j t -> p (j t)"),
             )
 
-        a_rows = []
+        a_banks = []
         for t in range(PACK):
-            rows = keep.tile([P, J], F32, name="a_rows%d" % t)
-            pieces = [slice(0, HJ), slice(HJ, J)] if t == 0 else [slice(0, J)]
-            for cols in pieces:
-                acc = bank()
+            acc = bank()
+            for h in range(2):
+                cols = slice(HJ * h, HJ * (h + 1))
                 nc.tensor.matmul_mx(
                     out=acc[:, cols],
                     lhsT=w_dealt[:, P * t : P * (t + 1)].bitcast(FP8X4),
@@ -213,7 +234,15 @@ def tile_picked_refined_plain_two_groupmeet_one_posted_kernel(
                     start=True,
                     stop=True,
                 )
-                nc.vector.tensor_copy(out=rows[:, cols], in_=acc[:, cols])
+            a_banks.append(acc)
+        for t in (2, 3):
+            rows = keep.tile([P, J], F32, name="b_rows%d" % t, tag="woven%d" % (3 - t), align_bytes=64)
+            nc.vector.tensor_copy(out=rows[:], in_=b_banks[t][:])
+            pick_b(t, rows)
+        a_rows = []
+        for t in range(PACK):
+            rows = keep.tile([P, J], F32, name="a_rows%d" % t)
+            nc.vector.tensor_copy(out=rows[:], in_=a_banks[t][:])
             a_rows.append(rows)
 
         HO = O // 2
@@ -235,7 +264,7 @@ def tile_picked_refined_plain_two_groupmeet_one_posted_kernel(
         hid = []
         for h in range(2):
             cols = slice(HO * h, HO * (h + 1))
-            tile = keep.tile([P, HO, PACK], BF16, name="hid%d" % h, tag=("xc_codes", "fine2")[h], align_bytes=64)
+            tile = keep.tile([P, HO, PACK], BF16, name="hid%d" % h, tag=("xc_codes", "xc_scales")[h], align_bytes=64)
             nc.vector.tensor_tensor(
                 out=tile[:, :, 0:2],
                 in0=a_low[:, :, cols].rearrange("p t o -> p o t"),
@@ -264,7 +293,7 @@ def tile_picked_refined_plain_two_groupmeet_one_posted_kernel(
                 nc.tensor.matmul_mx(
                     out=acc[:, 0:HO],
                     lhsT=wb_sb[:, 2 * P * c : 2 * P * (c + 1)].bitcast(FP4X4),
-                    lhsT_scale=w_plane[:, 2 * R + P * c : 2 * R + P * (c + 1)],
+                    lhsT_scale=wb_plane[:, P * c : P * (c + 1)],
                     rhs=codes[:].bitcast(FP8X4),
                     rhs_scale=scales[:],
                     start=True,

@@ -123,8 +123,8 @@ def tile_picked_refined_plain_two_groupmeet_one_posted_kernel(
         spread_scales(w_plane, w_stage)
         dealt_scales = keep.tile([P, 2, R], U8, name="dealt_scales", align_bytes=64)
         nc.vector.tensor_copy(
-            out=dealt_scales[:].rearrange("p s (t m) -> p s m t", t=PACK),
-            in_=w_plane[:].rearrange("p (s m t) -> p s m t", s=2, t=PACK),
+            out=dealt_scales[:].rearrange("p s (t m) -> p s t m", t=PACK),
+            in_=w_plane[:].rearrange("p (s m t) -> p s t m", s=2, t=PACK),
         )
 
         coarse, fine = [], []
@@ -139,8 +139,8 @@ def tile_picked_refined_plain_two_groupmeet_one_posted_kernel(
 
         w2_dealt = keep.tile([P, 2 * R], U8, name="w2_dealt", tag="w2_dealt", align_bytes=64)
         nc.scalar.copy(
-            out=w2_dealt[:].bitcast(U16).rearrange("p (t m) -> p m t", t=PACK),
-            in_=w2_raw[:].bitcast(U16).rearrange("p (m t) -> p m t", t=PACK),
+            out=w2_dealt[:].bitcast(U16).rearrange("p (t m) -> p t m", t=PACK),
+            in_=w2_raw[:].bitcast(U16).rearrange("p (m t) -> p t m", t=PACK),
         )
 
         HJ = J // 2
@@ -223,17 +223,15 @@ def tile_picked_refined_plain_two_groupmeet_one_posted_kernel(
         a_banks = []
         for t in range(PACK):
             acc = bank()
-            for h in range(2):
-                cols = slice(HJ * h, HJ * (h + 1))
-                nc.tensor.matmul_mx(
-                    out=acc[:, cols],
-                    lhsT=w_dealt[:, P * t : P * (t + 1)].bitcast(FP8X4),
-                    lhsT_scale=dealt_scales[:, 1, P * t : P * (t + 1)],
-                    rhs=xc_codes[:, cols].bitcast(FP8X4),
-                    rhs_scale=xc_scales[:, cols],
-                    start=True,
-                    stop=True,
-                )
+            nc.tensor.matmul_mx(
+                out=acc[:],
+                lhsT=w_dealt[:, P * t : P * (t + 1)].bitcast(FP8X4),
+                lhsT_scale=dealt_scales[:, 1, P * t : P * (t + 1)],
+                rhs=xc_codes[:].bitcast(FP8X4),
+                rhs_scale=xc_scales[:],
+                start=True,
+                stop=True,
+            )
             a_banks.append(acc)
         for t in (2, 3):
             rows = keep.tile([P, J], F32, name="b_rows%d" % t, tag="woven%d" % (3 - t), align_bytes=64)

from contextlib import ExitStack

import concourse.mybir as mybir

K, J, R, T, Z, M, O, N, U, E = 512, 512, 512, 2048, 512, 1024, 256, 256, 128, 512
FLOPS = 2 * (K * R * J + Z * R * J + R * N * O)

F32 = mybir.dt.float32
BF16 = mybir.dt.bfloat16
I32 = mybir.dt.int32
U32 = mybir.dt.uint32
U16 = mybir.dt.uint16
U8 = mybir.dt.uint8
FP8X4 = mybir.dt.float8_e4m3fn_x4
FP4X4 = mybir.dt.float4_e2m1fn_x4
COPY = mybir.ActivationFunctionType.Copy
ADD = mybir.AluOpType.add
MAX = mybir.AluOpType.max

P = 128
PACK = 4
QUADS = 4
BANK = 512


def tile_picked_refined_plain_two_groupmeet_one_posted_kernel(
    tc, ta, ga, gb, w_words, w_scales, xo_words, xo_scales, w2_words, w2_scales, sa, sb, wb_words, wb_scales, so,
    offs, offs2, offs3, offs4, offs5, offs6, offs7, out,
):
    nc = tc.nc
    with ExitStack() as ctx:
        lists = ctx.enter_context(tc.tile_pool(name="lists", bufs=1))
        keep = ctx.enter_context(tc.tile_pool(name="keep", bufs=1))
        last = ctx.enter_context(tc.tile_pool(name="last", bufs=1))
        psum = ctx.enter_context(tc.psum_pool(name="psum", bufs=8))

        def load_list(name, src):
            tile = lists.tile(list(src.shape), U16, name=name)
            nc.sync.dma_start(tile[:], src)
            return tile

        def load_dealt(queue, name, src):
            tile = keep.tile([P, PACK], F32, name=name)
            queue.dma_start(out=tile[:], in_=src.rearrange("(p t) o -> p (t o)", t=PACK))
            return tile

        ta_rows = ta.rearrange("(p t) c -> p t c", t=PACK)

        def load_table(t):
            if t == PACK - 1:
                tile = last.tile([P, T], F32, name="table%d" % t, offset=0)
            else:
                tile = keep.tile([P, T], F32, name="table%d" % t)
            nc.sync.dma_start(out=tile[:], in_=ta_rows[:, t, :])
            return tile

        def load_words(name, src, dtype, width):
            tile = keep.tile([P, width], dtype, name=name, align_bytes=64)
            nc.sync.dma_start(out=tile[:].bitcast(I32), in_=src.bitcast(I32))
            return tile

        def stage_scales(queues, stage, first, src):
            halves = len(queues)
            rows = src[0].bitcast(I32).rearrange("(u q i) n -> u i q n", u=halves, i=4)
            for u in range(halves):
                queues[u].dma_start(out=stage[64 * u : 64 * u + 4, :, first : first + rows.shape[3]], in_=rows[u])

        def spread_scales(plane, stage):
            held = stage.shape[1]
            for q in range(QUADS):
                first = 64 * (q // held)
                nc.vector.tensor_copy(
                    out=plane[32 * q : 32 * q + 4, :].bitcast(I32), in_=stage[first : first + 4, q % held, :]
                )

        def bank():
            return psum.tile([P, BANK], F32, name="bank")

        xo_stage = keep.tile([P, 2, M // 4], I32, name="xo_stage")
        stage_scales((nc.scalar, nc.scalar), xo_stage, 0, xo_scales)
        ga_sb = load_dealt(nc.scalar, "ga_sb", ga)
        gb_sb = load_dealt(nc.scalar, "gb_sb", gb)
        w2_raw = load_words("w2_raw", w2_words[0], U8, 2 * R)
        idx3 = load_list("idx3", offs3)
        idx = load_list("idx", offs)
        tables = [load_table(0)]
        idx2 = load_list("idx2", offs2)
        w_stage = keep.tile([P, 2, 2 * R // 4], I32, name="w_stage")
        stage_scales((nc.sync, nc.sync), w_stage, 0, w2_scales)
        stage_scales((nc.sync, nc.sync), w_stage, R // 4, w_scales)
        tables.append(load_table(1))
        wb_stage = keep.tile([P, QUADS, N // 4], I32, name="wb_stage", align_bytes=64)
        stage_scales((nc.sync,), wb_stage, 0, wb_scales)
        tables.extend(load_table(t) for t in (2, 3))
        xo_sb = load_words("xo_sb", xo_words[0].rearrange("p n t -> p (n t)"), U32, M)
        w_raw = load_words("w_raw", w_words[0].rearrange("p n t -> p (n t)"), U32, R)
        idx5 = load_list("idx5", offs5)
        sb_sb = load_dealt(nc.sync, "sb_sb", sb)
        idx4 = load_list("idx4", offs4)
        sa_sb = load_dealt(nc.sync, "sa_sb", sa)
        wb_sb = load_words("wb_sb", wb_words[0], U8, 2 * N)
        so_sb = keep.tile([P, N // P, 1], F32, name="so_sb")
        with nc.allow_non_contiguous_dma(reason="one value a partition for each block of 128 output features"):
            nc.sync.dma_start(out=so_sb[:], in_=so.rearrange("(c p) o -> p c o", p=P))
        idx6 = load_list("idx6", offs6)
        idx7 = load_list("idx7", offs7)

        def cleared_plane(name, width, tag):
            plane = keep.tile([P, width], U8, name=name, tag=tag, align_bytes=64)
            nc.vector.memset(plane[:].bitcast(I32), 0)
            return plane

        xo_plane = cleared_plane("xo_plane", M, "xo_plane")
        w_plane = cleared_plane("w_plane", 2 * R, "w_plane")
        pages = []
        for c in range(N // P):
            page = keep.tile([P, E], F32, name="page%d" % c)
            nc.vector.memset(page[:], 0.0)
            pages.append(page)
        spread_scales(xo_plane, xo_stage)
        note_scales = keep.tile([P, J], U8, name="note_scales", align_bytes=64)
        nc.vector.tensor_copy(out=note_scales[:], in_=xo_plane[:].indirect(idx3[:]))
        spread_scales(w_plane, w_stage)
        dealt_scales = keep.tile([P, 2, R], U8, name="dealt_scales", align_bytes=64)
        nc.vector.tensor_copy(
            out=dealt_scales[:].rearrange("p s (t m) -> p s t m", t=PACK),
            in_=w_plane[:].rearrange("p (s m t) -> p s t m", s=2, t=PACK),
        )

        coarse, fine = [], []

        def look_up(t):
            g1 = keep.tile([P, J], F32, name="coarse%d" % t, align_bytes=64)
            nc.scalar.activation(out=g1[:], in_=tables[t][:].indirect(idx[:]), func=COPY, scale=ga_sb[:, t : t + 1])
            g2 = keep.tile([P, J], F32, name="fine%d" % t, align_bytes=64)
            nc.scalar.activation(out=g2[:], in_=tables[t][:].indirect(idx2[:]), func=COPY, scale=gb_sb[:, t : t + 1])
            coarse.append(g1)
            fine.append(g2)

        w2_dealt = keep.tile([P, 2 * R], U8, name="w2_dealt", tag="w2_dealt", align_bytes=64)
        nc.scalar.copy(
            out=w2_dealt[:].bitcast(U16).rearrange("p (t m) -> p t m", t=PACK),
            in_=w2_raw[:].bitcast(U16).rearrange("p (m t) -> p t m", t=PACK),
        )

        HJ = J // 2
        xc_low = keep.tile([P, 2, J], BF16, name="xc_low", tag="relay", align_bytes=64)
        for t in (0, 1):
            look_up(t)
            nc.vector.tensor_tensor(out=xc_low[:, t, :], in0=coarse[t][:], in1=fine[t][:], op=ADD)
        woven = []
        for h in range(2):
            tile = keep.tile([P, HJ, PACK], BF16, name="woven%d" % h, align_bytes=64)
            nc.vector.tensor_copy(
                out=tile[:, :, 0:2], in_=xc_low[:, :, HJ * h : HJ * (h + 1)].rearrange("p t j -> p j t")
            )
            woven.append(tile)
        look_up(2)
        wb_plane = cleared_plane("wb_plane", N, "relay")
        spread_scales(wb_plane, wb_stage)
        xc_high = keep.tile([P, 2, J], BF16, name="xc_high")
        nc.vector.tensor_tensor(out=xc_high[:, 0, :], in0=coarse[2][:], in1=fine[2][:], op=ADD)
        note_codes = keep.tile([P, J], U32, name="note_codes", tag="fine2", align_bytes=64)
        for h in range(2):
            nc.vector.tensor_copy(
                out=note_codes[:, HJ * h : HJ * (h + 1)],
                in_=xo_sb[:].indirect(idx3[:, HJ // 16 * h : HJ // 16 * (h + 1)]),
            )
        look_up(3)
        w_dealt = last.tile([P, R], U32, name="w_dealt", offset=0, align_bytes=64)
        nc.scalar.copy(
            out=w_dealt[:].rearrange("p (t m) -> p m t", t=PACK),
            in_=w_raw[:].rearrange("p (m t) -> p m t", t=PACK),
        )

        b_banks = [bank() for t in range(PACK)]

        def b_product(t, cols):
            nc.tensor.matmul_mx(
                out=b_banks[t][:, cols],
                lhsT=w2_dealt[:, 2 * P * t : 2 * P * (t + 1)].bitcast(FP4X4),
                lhsT_scale=dealt_scales[:, 0, P * t : P * (t + 1)],
                rhs=note_codes[:, cols].bitcast(FP8X4),
                rhs_scale=note_scales[:, cols],
                start=True,
                stop=True,
            )

        for h in range(2):
            for t in (0, 1):
                b_product(t, slice(HJ * h, HJ * (h + 1)))
        for t in (2, 3):
            b_product(t, slice(0, J))
        b_picked = keep.tile([P, PACK, O], F32, name="b_picked")

        def pick_b(t, rows):
            nc.scalar.activation(
                out=b_picked[:, t, :], in_=rows[:].indirect(idx5[:]), func=COPY, scale=sb_sb[:, t : t + 1]
            )

        b_low = [last.tile([P, J], F32, name="b_rows%d" % t, offset=4 * (R + J * t)) for t in (0, 1)]
        for t in (0, 1):
            nc.scalar.copy(out=b_low[t][:], in_=b_banks[t][:])
        for t in (0, 1):
            pick_b(t, b_low[t])

        for h in range(2):
            cols = slice(HJ * h, HJ * (h + 1))
            nc.vector.tensor_tensor(out=xc_high[:, 1, cols], in0=coarse[3][:, cols], in1=fine[3][:, cols], op=ADD)
        for h in range(2):
            cols = slice(HJ * h, HJ * (h + 1))
            nc.vector.tensor_copy(out=woven[h][:, :, 2:4], in_=xc_high[:, :, cols].rearrange("p t j -> p j t"))
        xc_codes = keep.tile([P, J], U32, name="xc_codes", align_bytes=64)
        xc_scales = keep.tile([P, J], U8, name="xc_scales", align_bytes=64)
        for h in range(2):
            cols = slice(HJ * h, HJ * (h + 1))
            nc.vector.quantize_mx(
                out=xc_codes[:, cols].bitcast(FP8X4),
                scales=xc_scales[:, cols],
                in_=woven[h][:].rearrange("p j t -> p (j t)"),
            )

        a_banks = []
        for t in range(PACK):
            acc = bank()
            nc.tensor.matmul_mx(
                out=acc[:],
                lhsT=w_dealt[:, P * t : P * (t + 1)].bitcast(FP8X4),
                lhsT_scale=dealt_scales[:, 1, P * t : P * (t + 1)],
                rhs=xc_codes[:].bitcast(FP8X4),
                rhs_scale=xc_scales[:],
                start=True,
                stop=True,
            )
            a_banks.append(acc)
        for t in (2, 3):
            rows = keep.tile([P, J], F32, name="b_rows%d" % t, tag="woven%d" % (3 - t), align_bytes=64)
            nc.vector.tensor_copy(out=rows[:], in_=b_banks[t][:])
            pick_b(t, rows)
        a_rows = []
        for t in range(PACK):
            rows = keep.tile([P, J], F32, name="a_rows%d" % t)
            nc.vector.tensor_copy(out=rows[:], in_=a_banks[t][:])
            a_rows.append(rows)

        HO = O // 2
        a_low = keep.tile([P, 2, O], F32, name="a_low")
        for t in range(2):
            nc.scalar.activation(
                out=a_low[:, t, :], in_=a_rows[t][:].indirect(idx4[:]), func=COPY, scale=sa_sb[:, t : t + 1]
            )
        a_high = [keep.tile([P, 2, HO], F32, name="a_high%d" % h) for h in range(2)]
        for t in (2, 3):
            for h in range(2):
                nc.scalar.activation(
                    out=a_high[h][:, t - 2, :],
                    in_=a_rows[t][:].indirect(idx4[:, HO // 16 * h : HO // 16 * (h + 1)]),
                    func=COPY,
                    scale=sa_sb[:, t : t + 1],
                )

        hid = []
        for h in range(2):
            cols = slice(HO * h, HO * (h + 1))
            tile = keep.tile([P, HO, PACK], BF16, name="hid%d" % h, tag=("xc_codes", "xc_scales")[h], align_bytes=64)
            nc.vector.tensor_tensor(
                out=tile[:, :, 0:2],
                in0=a_low[:, :, cols].rearrange("p t o -> p o t"),
                in1=b_picked[:, 0:2, cols].rearrange("p t o -> p o t"),
                op=MAX,
            )
            hid.append(tile)
        for h in range(2):
            cols = slice(HO * h, HO * (h + 1))
            nc.vector.tensor_tensor(
                out=hid[h][:, :, 2:4],
                in0=a_high[h][:].rearrange("p t o -> p o t"),
                in1=b_picked[:, 2:4, cols].rearrange("p t o -> p o t"),
                op=MAX,
            )
        p_rows = [keep.tile([P, O], F32, name="p_rows%d" % c) for c in range(N // P)]
        p_banks = []
        for h in range(2):
            codes = keep.tile([P, HO], U32, name="hid_codes%d" % h, align_bytes=64)
            scales = keep.tile([P, HO], U8, name="hid_scales%d" % h, align_bytes=64)
            nc.vector.quantize_mx(
                out=codes[:].bitcast(FP8X4), scales=scales[:], in_=hid[h][:].rearrange("p o t -> p (o t)")
            )
            for c in range(N // P):
                acc = bank()
                nc.tensor.matmul_mx(
                    out=acc[:, 0:HO],
                    lhsT=wb_sb[:, 2 * P * c : 2 * P * (c + 1)].bitcast(FP4X4),
                    lhsT_scale=wb_plane[:, P * c : P * (c + 1)],
                    rhs=codes[:].bitcast(FP8X4),
                    rhs_scale=scales[:],
                    start=True,
                    stop=True,
                )
                p_banks.append(acc)
        for c in range(N // P):
            nc.scalar.copy(out=p_rows[c][:, 0:HO], in_=p_banks[c][:, 0:HO])
        for c in range(N // P):
            nc.vector.tensor_copy(out=p_rows[c][:, HO:O], in_=p_banks[2 + c][:, 0:HO])
        for c in range(N // P):
            ends = keep.tile([P, U], F32, name="ends%d" % c)
            nc.scalar.activation(out=ends[:], in_=p_rows[c][:].indirect(idx6[:]), func=COPY, scale=so_sb[:, c, :])
            nc.vector.tensor_copy(out=pages[c][:].indirect(idx7[:]), in_=ends[:])
            nc.sync.dma_start(out=out[P * c : P * (c + 1), :], in_=pages[c][:])
